import numpy as np, ml_dtypes
CORES = [8,136,40,168]
N = 4
import mx_ref
NC, D = 256, 3
SRC = [[1,2,3],[1,2,3],[1,2,3],[0,1,3]]
BF = ml_dtypes.bfloat16
def setup_inputs(rng):
    def f(*shape):
        return mx_ref.flush((rng.standard_normal(shape, dtype=np.float32) * np.exp2(rng.integers(-2, 3, shape[:-1] + (1,)))).astype(BF))
    return {"w": f(N, 128, D * 512), "x": f(N, 128, 4 * NC)}
def setup_inputs_blocks(rng):
    d = setup_inputs(rng)
    for k in ("w", "x"): d[k] = mx_ref.spread(d[k], rng, 1)
    return d
def setup_inputs_wide(rng):
    d = setup_inputs(rng)
    for k in ("w", "x"): d[k] = mx_ref.flush((d[k].astype(np.float32) * np.exp2(rng.integers(-8, 9, (N, 1, 1))).astype(np.float32)).astype(BF))
    return d
def setup_inputs_zeros(rng):
    d = setup_inputs(rng); v = d["x"].reshape(N, 128, -1, 4).copy()
    v[np.broadcast_to((rng.random((N, 1, v.shape[2], 1)) < 0.33), v.shape)] = 0
    d["x"] = v.reshape(d["x"].shape)
    return d
def reference(w, x):
    QX = [mx_ref.quantize(x[j]) for j in range(N)]
    y = np.zeros((N, 128, NC), np.float32)
    for r in range(N):
        for i in range(D):
            p = mx_ref.matmul(mx_ref.quantize(w[r][:, 512 * i:512 * i + 512]), QX[SRC[r][i]])
            y[r] = p if i == 0 else y[r] + p
    return {"y": y}

@@ -1,0 +1,125 @@
+from concourse.bass import DstId, RemoteDMATransfer
+from concourse.mybir import dt
+
+NC = 256
+MW = 128
+D = 3
+
+SCRATCH = {
+    "xb": ("sbuf", [128, 4 * NC], "bfloat16"),
+    "wb": ("sbuf", [128, 4 * MW * D], "bfloat16"),
+    "xc": ("sbuf", [128, NC], "float8_e4m3fn_x4"),
+    "xs": ("sbuf", [128, NC], "uint8"),
+    "wc": ("sbuf", [128, MW * D], "float8_e4m3fn_x4"),
+    "ws": ("sbuf", [128, MW * D], "uint8"),
+    "lc": ("sbuf", [128, NC * D], "float8_e4m3fn_x4"),
+    "ls": ("sbuf", [128, NC * D], "uint8"),
+    "acc": ("psum", [128, 512], "float32"),
+    "yb": ("sbuf", [128, NC], "float32"),
+}
+SEMAPHORES = ["xl", "wl", "xq", "wq", "a0", "a1", "a2", "a3", "sent", "mm", "cp", "st"]
+
+
+def _perms(items):
+    if len(items) <= 1:
+        return [list(items)]
+    out = []
+    for k in range(len(items)):
+        for rest in _perms(items[:k] + items[k + 1:]):
+            out.append([items[k]] + rest)
+    return out
+
+
+def _send_orders(src, n):
+    dests = [[r for r in range(n) if r != j and j in src[r]] for j in range(n)]
+    best = [None, None]
+
+    def walk(j, chosen, clashes):
+        if best[0] is not None and clashes >= best[0]:
+            return
+        if j == n:
+            best[0], best[1] = clashes, [list(c) for c in chosen]
+            return
+        for p in _perms(dests[j]):
+            more = 0
+            for turn, r in enumerate(p):
+                for c in chosen:
+                    if turn < len(c) and c[turn] == r:
+                        more += 1
+            walk(j + 1, chosen + [p], clashes + more)
+
+    walk(0, [], 0)
+    return best[1]
+
+
+def _engines(mask):
+    return bin(mask).count("1")
+
+
+def rank_program(g, core, T, topo):
+    rank = T.rank_of(core)
+    if rank is None:
+        return
+    src = T.tables["SRC"]
+    n = len(T.cores)
+    orders = _send_orders(src, n)
+    sem = T.sem
+
+    g.sync.dma_start(T.xb[:], T.x[:]).then_inc(sem.xl, 16)
+    g.sync.dma_start(T.wb[:], T.w[:]).then_inc(sem.wl, 16)
+
+    g.vector.wait_ge(sem.xl, 16)
+    g.vector.quantize_mx(T.xc[:], T.xs[:], T.xb[:]).then_inc(sem.xq, 1)
+    g.vector.wait_ge(sem.wl, 16)
+    for i in range(D):
+        g.vector.quantize_mx(T.wc[:, MW * i:MW * (i + 1)], T.ws[:, MW * i:MW * (i + 1)],
+                             T.wb[:, 4 * MW * i:4 * MW * (i + 1)]).then_inc(sem.wq, 1)
+
+    g.wait_ge(sem.xq, 1)
+    mine = orders[rank]
+    left = 0
+    if mine:
+        mask = topo.mask(core, T.cores[mine[0]])
+        ids, slots = [], []
+        for r in mine:
+            d = T.cores[r]
+            mask &= topo.mask(core, d)
+            rid, pid = topo.addr(d, core)
+            ids.append(DstId(rid=rid, pnc=pid))
+            slots.append(src[r].index(rank))
+        arrive = sem["a%d" % rank]
+        g.remote_dma_fused([RemoteDMATransfer(
+            dst_ids=ids, dma_engine_mask=mask, remote_sem=arrive, srcs=[T.xs[:]],
+            dsts=[T.ls[:, NC * i:NC * (i + 1)] for i in slots])], local_sem=sem.sent)
+        g.remote_dma_fused([RemoteDMATransfer(
+            dst_ids=ids, dma_engine_mask=mask, remote_sem=arrive, srcs=[T.xc[:].bitcast(dt.uint8)],
+            dsts=[T.lc[:, NC * i:NC * (i + 1)].bitcast(dt.uint8) for i in slots])], local_sem=sem.sent)
+        left = 2 * _engines(mask)
+
+    def when(i):
+        j = src[rank][i]
+        return (-1, 0) if j == rank else (orders[j].index(rank), len(orders[j]))
+
+    todo = sorted(range(D), key=when)
+    g.tensor.wait_ge(sem.wq, D)
+    for k, i in enumerate(todo):
+        j = src[rank][i]
+        if j == rank:
+            g.tensor.wait_ge(sem.xq, 1)
+            codes, plane = T.xc[:], T.xs[:]
+        else:
+            g.tensor.wait_ge(sem["a%d" % j], 2 * _engines(topo.mask(T.cores[j], core)))
+            codes, plane = T.lc[:, NC * i:NC * (i + 1)], T.ls[:, NC * i:NC * (i + 1)]
+        mm = g.tensor.matmul_mx(T.acc[:, 0:NC], T.wc[:, MW * i:MW * (i + 1)], T.ws[:, MW * i:MW * (i + 1)],
+                                codes, plane, k == 0, k == D - 1)
+        if k == D - 1:
+            mm.then_inc(sem.mm, 1)
+
+    g.vector.wait_ge(sem.mm, 1)
+    g.vector.tensor_copy(T.yb[:], T.acc[:, 0:NC]).then_inc(sem.cp, 1)
+    g.sync.wait_ge(sem.cp, 1)
+    g.sync.dma_start(T.y[:], T.yb[:]).then_inc(sem.st, 16)
+    g.sync.wait_ge(sem.st, 16)
+
+    if left:
+        g.wait_ge(sem.sent, left)

@@ -4,6 +4,8 @@ from concourse.mybir import dt
 NC = 256
 MW = 128
 D = 3
+WORLD = 256
+SHARE = 2
 
 SCRATCH = {
     "xb": ("sbuf", [128, 4 * NC], "bfloat16"),
@@ -17,7 +19,7 @@ SCRATCH = {
     "acc": ("psum", [128, 512], "float32"),
     "yb": ("sbuf", [128, NC], "float32"),
 }
-SEMAPHORES = ["xl", "wl", "xq", "wq", "a0", "a1", "a2", "a3", "sent", "mm", "cp", "st"]
+SEMAPHORES = ["xl", "wl", "xq", "wq", "a0", "a1", "a2", "a3", "sent", "hp", "mm", "cp", "st"]
 
 
 def _perms(items):
@@ -56,14 +58,69 @@ def _engines(mask):
     return bin(mask).count("1")
 
 
+def _same_chip(a, b, topo):
+    return topo.host(a) == topo.host(b) and topo.chip(a) == topo.chip(b)
+
+
+def _plane_plan(j, order, T, topo):
+    if len(order) < 2:
+        return []
+    c = T.cores[j]
+    free = [h for h in range(WORLD) if _same_chip(h, c, topo) and topo.die(h) != topo.die(c) and T.rank_of(h) is None
+            and all(topo.may_write(h, T.cores[r]) for r in order)]
+    return [(free[k // SHARE], order[k:k + SHARE]) for k in range(0, len(order), SHARE)]
+
+
+def _dests(sender, j, ranks, T, topo):
+    mask = topo.mask(sender, T.cores[ranks[0]])
+    ids, slots = [], []
+    for r in ranks:
+        d = T.cores[r]
+        mask &= topo.mask(sender, d)
+        rid, pid = topo.addr(d, sender)
+        ids.append(DstId(rid=rid, pnc=pid))
+        slots.append(T.tables["SRC"][r].index(j))
+    return ids, slots, mask
+
+
+def _plane_writes(sender, j, ranks, T, topo):
+    ids, slots, mask = _dests(sender, j, ranks, T, topo)
+    return [RemoteDMATransfer(
+        dst_ids=ids, dma_engine_mask=mask, remote_sem=T.sem["a%d" % j], srcs=[T.xs[:]],
+        dsts=[T.ls[:, NC * i:NC * (i + 1)] for i in slots])], _engines(mask)
+
+
+def _relay_mask(c, helpers, order, T, topo):
+    m = topo.mask(c, helpers[0])
+    for h in helpers:
+        m &= topo.mask(c, h)
+    for r in order:
+        m &= ~topo.mask(c, T.cores[r])
+    return m
+
+
 def rank_program(g, core, T, topo):
     rank = T.rank_of(core)
-    if rank is None:
-        return
     src = T.tables["SRC"]
     n = len(T.cores)
-    orders = _send_orders(src, n)
     sem = T.sem
+
+    if rank is None:
+        owners = [j for j in range(n) if _same_chip(T.cores[j], core, topo)]
+        if not owners:
+            return
+        orders = _send_orders(src, n)
+        for j in owners:
+            plan = _plane_plan(j, orders[j], T, topo)
+            for h, ranks in plan:
+                if h == core:
+                    g.wait_ge(sem.hp, _engines(_relay_mask(T.cores[j], [p[0] for p in plan], orders[j], T, topo)))
+                    writes, k = _plane_writes(core, j, ranks, T, topo)
+                    g.remote_dma_fused(writes, local_sem=sem.sent)
+                    g.wait_ge(sem.sent, k)
+        return
+
+    orders = _send_orders(src, n)
 
     g.sync.dma_start(T.xb[:], T.x[:]).then_inc(sem.xl, 16)
     g.sync.dma_start(T.wb[:], T.w[:]).then_inc(sem.wl, 16)
@@ -79,22 +136,24 @@ def rank_program(g, core, T, topo):
     mine = orders[rank]
     left = 0
     if mine:
-        mask = topo.mask(core, T.cores[mine[0]])
-        ids, slots = [], []
-        for r in mine:
-            d = T.cores[r]
-            mask &= topo.mask(core, d)
-            rid, pid = topo.addr(d, core)
-            ids.append(DstId(rid=rid, pnc=pid))
-            slots.append(src[r].index(rank))
-        arrive = sem["a%d" % rank]
+        plan = _plane_plan(rank, mine, T, topo)
+        if plan:
+            helpers = [p[0] for p in plan]
+            hm = _relay_mask(core, helpers, mine, T, topo)
+            hid = [topo.addr(h, core) for h in helpers]
+            g.remote_dma_fused([RemoteDMATransfer(
+                dst_ids=[DstId(rid=a[0], pnc=a[1]) for a in hid], dma_engine_mask=hm, remote_sem=sem.hp,
+                srcs=[T.xs[:]], dsts=[T.xs[:] for h in helpers])], local_sem=sem.sent)
+            left += _engines(hm)
+        else:
+            writes, k = _plane_writes(core, rank, mine, T, topo)
+            g.remote_dma_fused(writes, local_sem=sem.sent)
+            left += k
+        ids, slots, mask = _dests(core, rank, mine, T, topo)
         g.remote_dma_fused([RemoteDMATransfer(
-            dst_ids=ids, dma_engine_mask=mask, remote_sem=arrive, srcs=[T.xs[:]],
-            dsts=[T.ls[:, NC * i:NC * (i + 1)] for i in slots])], local_sem=sem.sent)
-        g.remote_dma_fused([RemoteDMATransfer(
-            dst_ids=ids, dma_engine_mask=mask, remote_sem=arrive, srcs=[T.xc[:].bitcast(dt.uint8)],
+            dst_ids=ids, dma_engine_mask=mask, remote_sem=sem["a%d" % rank], srcs=[T.xc[:].bitcast(dt.uint8)],
             dsts=[T.lc[:, NC * i:NC * (i + 1)].bitcast(dt.uint8) for i in slots])], local_sem=sem.sent)
-        left = 2 * _engines(mask)
+        left += _engines(mask)
 
     def when(i):
         j = src[rank][i]

from concourse.bass import DstId, RemoteDMATransfer
from concourse.mybir import dt

NC = 256
MW = 128
D = 3
WORLD = 256
SHARE = 2

SCRATCH = {
    "xb": ("sbuf", [128, 4 * NC], "bfloat16"),
    "wb": ("sbuf", [128, 4 * MW * D], "bfloat16"),
    "xc": ("sbuf", [128, NC], "float8_e4m3fn_x4"),
    "xs": ("sbuf", [128, NC], "uint8"),
    "wc": ("sbuf", [128, MW * D], "float8_e4m3fn_x4"),
    "ws": ("sbuf", [128, MW * D], "uint8"),
    "lc": ("sbuf", [128, NC * D], "float8_e4m3fn_x4"),
    "ls": ("sbuf", [128, NC * D], "uint8"),
    "acc": ("psum", [128, 512], "float32"),
    "yb": ("sbuf", [128, NC], "float32"),
}
SEMAPHORES = ["xl", "wl", "xq", "wq", "a0", "a1", "a2", "a3", "sent", "hp", "mm", "cp", "st"]


def _perms(items):
    if len(items) <= 1:
        return [list(items)]
    out = []
    for k in range(len(items)):
        for rest in _perms(items[:k] + items[k + 1:]):
            out.append([items[k]] + rest)
    return out


def _send_orders(src, n):
    dests = [[r for r in range(n) if r != j and j in src[r]] for j in range(n)]
    best = [None, None]

    def walk(j, chosen, clashes):
        if best[0] is not None and clashes >= best[0]:
            return
        if j == n:
            best[0], best[1] = clashes, [list(c) for c in chosen]
            return
        for p in _perms(dests[j]):
            more = 0
            for turn, r in enumerate(p):
                for c in chosen:
                    if turn < len(c) and c[turn] == r:
                        more += 1
            walk(j + 1, chosen + [p], clashes + more)

    walk(0, [], 0)
    return best[1]


def _engines(mask):
    return bin(mask).count("1")


def _same_chip(a, b, topo):
    return topo.host(a) == topo.host(b) and topo.chip(a) == topo.chip(b)


def _plane_plan(j, order, T, topo):
    if len(order) < 2:
        return []
    c = T.cores[j]
    free = [h for h in range(WORLD) if _same_chip(h, c, topo) and topo.die(h) != topo.die(c) and T.rank_of(h) is None
            and all(topo.may_write(h, T.cores[r]) for r in order)]
    return [(free[k // SHARE], order[k:k + SHARE]) for k in range(0, len(order), SHARE)]


def _dests(sender, j, ranks, T, topo):
    mask = topo.mask(sender, T.cores[ranks[0]])
    ids, slots = [], []
    for r in ranks:
        d = T.cores[r]
        mask &= topo.mask(sender, d)
        rid, pid = topo.addr(d, sender)
        ids.append(DstId(rid=rid, pnc=pid))
        slots.append(T.tables["SRC"][r].index(j))
    return ids, slots, mask


def _plane_writes(sender, j, ranks, T, topo):
    ids, slots, mask = _dests(sender, j, ranks, T, topo)
    return [RemoteDMATransfer(
        dst_ids=ids, dma_engine_mask=mask, remote_sem=T.sem["a%d" % j], srcs=[T.xs[:]],
        dsts=[T.ls[:, NC * i:NC * (i + 1)] for i in slots])], _engines(mask)


def _relay_mask(c, helpers, order, T, topo):
    m = topo.mask(c, helpers[0])
    for h in helpers:
        m &= topo.mask(c, h)
    for r in order:
        m &= ~topo.mask(c, T.cores[r])
    return m


def rank_program(g, core, T, topo):
    rank = T.rank_of(core)
    src = T.tables["SRC"]
    n = len(T.cores)
    sem = T.sem

    if rank is None:
        owners = [j for j in range(n) if _same_chip(T.cores[j], core, topo)]
        if not owners:
            return
        orders = _send_orders(src, n)
        for j in owners:
            plan = _plane_plan(j, orders[j], T, topo)
            for h, ranks in plan:
                if h == core:
                    g.wait_ge(sem.hp, _engines(_relay_mask(T.cores[j], [p[0] for p in plan], orders[j], T, topo)))
                    writes, k = _plane_writes(core, j, ranks, T, topo)
                    g.remote_dma_fused(writes, local_sem=sem.sent)
                    g.wait_ge(sem.sent, k)
        return

    orders = _send_orders(src, n)

    g.sync.dma_start(T.xb[:], T.x[:]).then_inc(sem.xl, 16)
    g.sync.dma_start(T.wb[:], T.w[:]).then_inc(sem.wl, 16)

    g.vector.wait_ge(sem.xl, 16)
    g.vector.quantize_mx(T.xc[:], T.xs[:], T.xb[:]).then_inc(sem.xq, 1)
    g.vector.wait_ge(sem.wl, 16)
    for i in range(D):
        g.vector.quantize_mx(T.wc[:, MW * i:MW * (i + 1)], T.ws[:, MW * i:MW * (i + 1)],
                             T.wb[:, 4 * MW * i:4 * MW * (i + 1)]).then_inc(sem.wq, 1)

    g.wait_ge(sem.xq, 1)
    mine = orders[rank]
    left = 0
    if mine:
        plan = _plane_plan(rank, mine, T, topo)
        if plan:
            helpers = [p[0] for p in plan]
            hm = _relay_mask(core, helpers, mine, T, topo)
            hid = [topo.addr(h, core) for h in helpers]
            g.remote_dma_fused([RemoteDMATransfer(
                dst_ids=[DstId(rid=a[0], pnc=a[1]) for a in hid], dma_engine_mask=hm, remote_sem=sem.hp,
                srcs=[T.xs[:]], dsts=[T.xs[:] for h in helpers])], local_sem=sem.sent)
            left += _engines(hm)
        else:
            writes, k = _plane_writes(core, rank, mine, T, topo)
            g.remote_dma_fused(writes, local_sem=sem.sent)
            left += k
        ids, slots, mask = _dests(core, rank, mine, T, topo)
        g.remote_dma_fused([RemoteDMATransfer(
            dst_ids=ids, dma_engine_mask=mask, remote_sem=sem["a%d" % rank], srcs=[T.xc[:].bitcast(dt.uint8)],
            dsts=[T.lc[:, NC * i:NC * (i + 1)].bitcast(dt.uint8) for i in slots])], local_sem=sem.sent)
        left += _engines(mask)

    def when(i):
        j = src[rank][i]
        return (-1, 0) if j == rank else (orders[j].index(rank), len(orders[j]))

    todo = sorted(range(D), key=when)
    g.tensor.wait_ge(sem.wq, D)
    for k, i in enumerate(todo):
        j = src[rank][i]
        if j == rank:
            g.tensor.wait_ge(sem.xq, 1)
            codes, plane = T.xc[:], T.xs[:]
        else:
            g.tensor.wait_ge(sem["a%d" % j], 2 * _engines(topo.mask(T.cores[j], core)))
            codes, plane = T.lc[:, NC * i:NC * (i + 1)], T.ls[:, NC * i:NC * (i + 1)]
        mm = g.tensor.matmul_mx(T.acc[:, 0:NC], T.wc[:, MW * i:MW * (i + 1)], T.ws[:, MW * i:MW * (i + 1)],
                                codes, plane, k == 0, k == D - 1)
        if k == D - 1:
            mm.then_inc(sem.mm, 1)

    g.vector.wait_ge(sem.mm, 1)
    g.vector.tensor_copy(T.yb[:], T.acc[:, 0:NC]).then_inc(sem.cp, 1)
    g.sync.wait_ge(sem.cp, 1)
    g.sync.dma_start(T.y[:], T.yb[:]).then_inc(sem.st, 16)
    g.sync.wait_ge(sem.st, 16)

    if left:
        g.wait_ge(sem.sent, left)
